import numpy as np
CORES = [7,135,263,391,15,143,271,399,23,151,279,407,31,159,287,415]
N = 16
GROUPS = [[0,1,2,3],[4,5,6,7],[8,9,10,11],[12,13,14,15]]
def setup_inputs(rng):
    return {"x": rng.standard_normal((N, 128, 4), dtype=np.float32)}
def reference(x):
    y = np.empty((N, 128, 4), x.dtype)
    for g in GROUPS:
        n = len(g); b = x.shape[2] // n
        for i, r in enumerate(g):
            y[r] = np.concatenate([x[s][:, i * b:(i + 1) * b] for s in g], axis=1)
    return {"y": y}

@@ -1,0 +1,67 @@
+from concourse.bass import DstId, RemoteDMATransfer
+
+SCRATCH = {
+    "xs": ("sbuf", [128, 4], "float32"),
+    "hop": ("sbuf", [128, 1], "float32"),
+    "out": ("sbuf", [128, 4], "float32"),
+}
+SEMAPHORES = ["loaded", "hopped", "filled", "sent", "stored"]
+
+M_HOP, M_NEAR, M_FAR, M_ALL = 0x0F, 0x30, 0xC0, 0xFF
+N_HOP, N_NEAR, N_FAR, N_ALL = 4, 2, 2, 8
+
+
+def rank_program(g, core, T, topo):
+    rank = T.rank_of(core)
+    if rank is None:
+        return
+    group = [m for m in T.tables["GROUPS"] if rank in m][0]
+    me = group.index(rank)
+    b = T.x.shape[1] // len(group)
+
+    near = far = diag = None
+    for i, r in enumerate(group):
+        c = T.cores[r]
+        if i == me:
+            continue
+        if not topo.may_write(core, c):
+            diag = i
+        elif topo.rack(topo.host(c)) == topo.rack(topo.host(core)):
+            near = i
+        else:
+            far = i
+
+    def blk(t, i):
+        return t[:, i * b:(i + 1) * b]
+
+    def dst(i):
+        rid, pid = topo.addr(T.cores[group[i]], core)
+        return DstId(rid=rid, pnc=pid)
+
+    g.sync.dma_start(T.xs[:], T.x[:]).then_inc(T.sem.loaded, 16)
+
+    g.scalar.wait_ge(T.sem.loaded, 16)
+    g.scalar.dma_start(blk(T.out, me), blk(T.xs, me)).then_inc(T.sem.filled, 16)
+
+    g.wait_ge(T.sem.loaded, 16)
+    g.remote_dma_fused(
+        [
+            RemoteDMATransfer(dst_ids=[dst(near)], dma_engine_mask=M_HOP, remote_sem=T.sem.hopped,
+                              src=blk(T.xs, diag), dst=T.hop[:]),
+            RemoteDMATransfer(dst_ids=[dst(near)], dma_engine_mask=M_NEAR, remote_sem=T.sem.filled,
+                              src=blk(T.xs, near), dst=blk(T.out, me)),
+            RemoteDMATransfer(dst_ids=[dst(far)], dma_engine_mask=M_FAR, remote_sem=T.sem.filled,
+                              src=blk(T.xs, far), dst=blk(T.out, me)),
+        ],
+        local_sem=T.sem.sent,
+    )
+
+    g.wait_ge(T.sem.hopped, N_HOP)
+    rid, pid = topo.addr(T.cores[group[far]], core)
+    g.remote_dma(blk(T.out, near), T.hop[:], T.sem.filled, T.sem.sent, pid, rid, M_ALL)
+
+    g.sync.wait_ge(T.sem.filled, 16 + N_NEAR + N_FAR + N_ALL)
+    g.sync.dma_start(T.y[:], T.out[:]).then_inc(T.sem.stored, 16)
+
+    g.wait_ge(T.sem.sent, N_HOP + N_NEAR + N_FAR + N_ALL)
+    g.wait_ge(T.sem.stored, 16)

@@ -1,14 +1,10 @@
-from concourse.bass import DstId, RemoteDMATransfer
-
 SCRATCH = {
-    "xs": ("sbuf", [128, 4], "float32"),
-    "hop": ("sbuf", [128, 1], "float32"),
+    "w": ("sbuf", [128, 6], "float32"),
     "out": ("sbuf", [128, 4], "float32"),
 }
-SEMAPHORES = ["loaded", "hopped", "filled", "sent", "stored"]
+SEMAPHORES = ["loaded", "got", "filled", "sent", "stored"]
 
-M_HOP, M_NEAR, M_FAR, M_ALL = 0x0F, 0x30, 0xC0, 0xFF
-N_HOP, N_NEAR, N_FAR, N_ALL = 4, 2, 2, 8
+MASK, ENGINES = 0xFF, 8
 
 
 def rank_program(g, core, T, topo):
@@ -19,49 +15,50 @@ def rank_program(g, core, T, topo):
     me = group.index(rank)
     b = T.x.shape[1] // len(group)
 
-    near = far = diag = None
+    near = far = None
     for i, r in enumerate(group):
         c = T.cores[r]
-        if i == me:
-            continue
-        if not topo.may_write(core, c):
-            diag = i
-        elif topo.rack(topo.host(c)) == topo.rack(topo.host(core)):
-            near = i
-        else:
-            far = i
+        if i != me and topo.may_write(core, c):
+            if topo.rack(topo.host(c)) == topo.rack(topo.host(core)):
+                near = i
+            else:
+                far = i
+    assert near == me ^ 1 and far == 3 - me
 
-    def blk(t, i):
-        return t[:, i * b:(i + 1) * b]
+    def cols(t, first, n):
+        return t[:, first * b:(first + n) * b]
 
-    def dst(i):
-        rid, pid = topo.addr(T.cores[group[i]], core)
-        return DstId(rid=rid, pnc=pid)
+    lower = me < near
+    mine, theirs = me & ~1, far & ~1
+    if lower:
+        at_mine, at_theirs, at_me, at_a = 0, 2, 0, 5
+        read1, read2, land1 = 1, 3, 0
+    else:
+        at_mine, at_theirs, at_me, at_a = 4, 2, 5, 0
+        read1, read2, land1 = 3, 1, 4
 
-    g.sync.dma_start(T.xs[:], T.x[:]).then_inc(T.sem.loaded, 16)
+    if at_mine - at_theirs == mine - theirs:
+        g.sync.dma_start(cols(T.w, min(at_mine, at_theirs), 4), T.x[:]).then_inc(T.sem.loaded, 16)
+        n_loaded = 16
+    else:
+        g.sync.dma_start(cols(T.w, at_theirs, 2), cols(T.x, theirs, 2)).then_inc(T.sem.loaded, 16)
+        g.scalar.dma_start(cols(T.w, at_mine, 2), cols(T.x, mine, 2)).then_inc(T.sem.loaded, 16)
+        n_loaded = 32
 
-    g.scalar.wait_ge(T.sem.loaded, 16)
-    g.scalar.dma_start(blk(T.out, me), blk(T.xs, me)).then_inc(T.sem.filled, 16)
+    g.wait_ge(T.sem.loaded, n_loaded)
+    rid, pid = topo.addr(T.cores[group[near]], core)
+    g.remote_dma(cols(T.w, land1, 2), cols(T.w, read1, 2), T.sem.got, T.sem.sent, pid, rid, MASK)
+    g.scalar.wait_ge(T.sem.loaded, n_loaded)
+    g.scalar.dma_start(cols(T.out, me, 1), cols(T.w, at_me, 1)).then_inc(T.sem.filled, 16)
 
-    g.wait_ge(T.sem.loaded, 16)
-    g.remote_dma_fused(
-        [
-            RemoteDMATransfer(dst_ids=[dst(near)], dma_engine_mask=M_HOP, remote_sem=T.sem.hopped,
-                              src=blk(T.xs, diag), dst=T.hop[:]),
-            RemoteDMATransfer(dst_ids=[dst(near)], dma_engine_mask=M_NEAR, remote_sem=T.sem.filled,
-                              src=blk(T.xs, near), dst=blk(T.out, me)),
-            RemoteDMATransfer(dst_ids=[dst(far)], dma_engine_mask=M_FAR, remote_sem=T.sem.filled,
-                              src=blk(T.xs, far), dst=blk(T.out, me)),
-        ],
-        local_sem=T.sem.sent,
-    )
-
-    g.wait_ge(T.sem.hopped, N_HOP)
+    g.wait_ge(T.sem.got, ENGINES)
     rid, pid = topo.addr(T.cores[group[far]], core)
-    g.remote_dma(blk(T.out, near), T.hop[:], T.sem.filled, T.sem.sent, pid, rid, M_ALL)
+    g.remote_dma(cols(T.out, mine, 2), cols(T.w, read2, 2), T.sem.filled, T.sem.sent, pid, rid, MASK)
+    g.scalar.wait_ge(T.sem.got, ENGINES)
+    g.scalar.dma_start(cols(T.out, near, 1), cols(T.w, at_a, 1)).then_inc(T.sem.filled, 16)
 
-    g.sync.wait_ge(T.sem.filled, 16 + N_NEAR + N_FAR + N_ALL)
+    g.sync.wait_ge(T.sem.filled, 16 + 16 + ENGINES)
     g.sync.dma_start(T.y[:], T.out[:]).then_inc(T.sem.stored, 16)
 
-    g.wait_ge(T.sem.sent, N_HOP + N_NEAR + N_FAR + N_ALL)
+    g.wait_ge(T.sem.sent, 2 * ENGINES)
     g.wait_ge(T.sem.stored, 16)

SCRATCH = {
    "w": ("sbuf", [128, 6], "float32"),
    "out": ("sbuf", [128, 4], "float32"),
}
SEMAPHORES = ["loaded", "got", "filled", "sent", "stored"]

MASK, ENGINES = 0xFF, 8


def rank_program(g, core, T, topo):
    rank = T.rank_of(core)
    if rank is None:
        return
    group = [m for m in T.tables["GROUPS"] if rank in m][0]
    me = group.index(rank)
    b = T.x.shape[1] // len(group)

    near = far = None
    for i, r in enumerate(group):
        c = T.cores[r]
        if i != me and topo.may_write(core, c):
            if topo.rack(topo.host(c)) == topo.rack(topo.host(core)):
                near = i
            else:
                far = i
    assert near == me ^ 1 and far == 3 - me

    def cols(t, first, n):
        return t[:, first * b:(first + n) * b]

    lower = me < near
    mine, theirs = me & ~1, far & ~1
    if lower:
        at_mine, at_theirs, at_me, at_a = 0, 2, 0, 5
        read1, read2, land1 = 1, 3, 0
    else:
        at_mine, at_theirs, at_me, at_a = 4, 2, 5, 0
        read1, read2, land1 = 3, 1, 4

    if at_mine - at_theirs == mine - theirs:
        g.sync.dma_start(cols(T.w, min(at_mine, at_theirs), 4), T.x[:]).then_inc(T.sem.loaded, 16)
        n_loaded = 16
    else:
        g.sync.dma_start(cols(T.w, at_theirs, 2), cols(T.x, theirs, 2)).then_inc(T.sem.loaded, 16)
        g.scalar.dma_start(cols(T.w, at_mine, 2), cols(T.x, mine, 2)).then_inc(T.sem.loaded, 16)
        n_loaded = 32

    g.wait_ge(T.sem.loaded, n_loaded)
    rid, pid = topo.addr(T.cores[group[near]], core)
    g.remote_dma(cols(T.w, land1, 2), cols(T.w, read1, 2), T.sem.got, T.sem.sent, pid, rid, MASK)
    g.scalar.wait_ge(T.sem.loaded, n_loaded)
    g.scalar.dma_start(cols(T.out, me, 1), cols(T.w, at_me, 1)).then_inc(T.sem.filled, 16)

    g.wait_ge(T.sem.got, ENGINES)
    rid, pid = topo.addr(T.cores[group[far]], core)
    g.remote_dma(cols(T.out, mine, 2), cols(T.w, read2, 2), T.sem.filled, T.sem.sent, pid, rid, MASK)
    g.scalar.wait_ge(T.sem.got, ENGINES)
    g.scalar.dma_start(cols(T.out, near, 1), cols(T.w, at_a, 1)).then_inc(T.sem.filled, 16)

    g.sync.wait_ge(T.sem.filled, 16 + 16 + ENGINES)
    g.sync.dma_start(T.y[:], T.out[:]).then_inc(T.sem.stored, 16)

    g.wait_ge(T.sem.sent, 2 * ENGINES)
    g.wait_ge(T.sem.stored, 16)
